import numpy as np
import ml_dtypes


def mxq(x, axis, fmt="e4m3"):
    dtype, down = {"e4m3": (ml_dtypes.float8_e4m3fn, 7), "e5m2": (ml_dtypes.float8_e5m2, 14)}[fmt]
    v = np.moveaxis(np.asarray(x, np.float32).astype(ml_dtypes.bfloat16).astype(np.float64), axis, -1)
    blocks = v.reshape(v.shape[:-1] + (-1, 32))
    amax = np.abs(blocks).max(-1, keepdims=True)
    byte = np.maximum(np.where(amax > 0, np.frexp(amax)[1] - 1 + 127, 0) - down, 1)
    scale = np.exp2(byte - 127.0)
    codes = (blocks / scale).astype(np.float32).astype(dtype).astype(np.float64)
    return np.moveaxis((codes * scale).reshape(v.shape), -1, axis)


WIDE = False


def mx_kscale(k):
    if not WIDE:
        return np.ones(k)
    levels = np.array([10, -10, 5, -5, 0])
    if k % 512:
        return np.exp2(np.random.permutation(np.resize(levels, k // 32))).repeat(32)
    a = np.empty((k // 512, 16))
    for p in range(k // 512):
        a[p, :8] = np.random.permutation(np.resize(levels, 8))
        for g in range(8):
            far = levels[np.abs(levels - a[p, g]) >= 10]
            a[p, g + 8] = far[np.random.randint(len(far))]
    return np.exp2(a.ravel()).repeat(32)


BF16 = ml_dtypes.bfloat16


def bf(x):
    return np.asarray(x, np.float32).astype(BF16)


def f64(x):
    return np.asarray(x).astype(np.float64)

def planes(Y):
    n, m = Y.shape
    b = f64(bf(Y)).reshape(n // 32, 32, m)
    amax = np.abs(b).max(1)
    byte = np.clip(np.where(amax > 0, np.frexp(amax)[1] - 1 + 127 - 7, 1), 1, 254)
    codes = (b * np.exp2(127.0 - byte)[:, None, :]).reshape(n, m).astype(np.float32).astype(ml_dtypes.float8_e4m3fn).view(np.uint8)
    words = codes.reshape(n // 512, 128, 4, m).transpose(0, 1, 3, 2)
    return np.ascontiguousarray(words), np.ascontiguousarray(byte.astype(np.uint8).reshape(n // 512, 16, m))


M, K, P, N = 1024, 512, 512, 1024


def basket_payoff(zq, a, k):
    return np.maximum((zq @ mxq(f64(a), 0, "e4m3")) + f64(k)[None, :], 0.0)


def path_scores(zq, u, q):
    return (zq @ mxq(f64(u), 0, "e4m3")) * f64(q)[:, None]


def setup_inputs():
    s, t = mx_kscale(K), mx_kscale(M)
    return {"z": bf(np.random.standard_normal((M, K)) * s),
            "a": bf(np.random.standard_normal((K, P)) / np.sqrt(K) / s[:, None]),
            "k": bf(np.random.standard_normal(P) * 0.3),
            "d": bf((1.0 + 0.1 * np.random.standard_normal(M)) * t),
            "u": bf(np.random.standard_normal((K, N)) / np.sqrt(K) / s[:, None]),
            "q": bf((1.0 + 0.1 * np.random.standard_normal(M)) / t)}


def core(z, a, k, d, u, q):
    zq = mxq(f64(z), 1, "e4m3")
    pay = basket_payoff(zq, a, k)
    b = (pay - np.mean(pay, axis=0, keepdims=True)) * f64(d)[:, None]
    sc = path_scores(zq, u, q)
    return (mxq(b.T, 1, "e4m3") @ mxq(sc, 0, "e4m3")) / np.sqrt(z.shape[0])


def reference(z, a, k, d, u, q):
    R_out = core(z, a, k, d, u, q)
    words, scales = planes(R_out.T)
    return R_out, words, scales

@@ -1,0 +1,466 @@
+from contextlib import ExitStack
+
+import concourse.mybir as mybir
+from concourse.masks import make_identity
+
+M, K, P, N = 1024, 512, 512, 1024
+FLOPS = 2 * M * K * (P + N) + 2 * P * M * N
+
+F32 = mybir.dt.float32
+BF16 = mybir.dt.bfloat16
+I32 = mybir.dt.int32
+U32 = mybir.dt.uint32
+U8 = mybir.dt.uint8
+FP8X4 = mybir.dt.float8_e4m3fn_x4
+ALU = mybir.AluOpType
+ACT = mybir.ActivationFunctionType
+
+ORDER = [
+    ("load", "a", 0),
+    ("load", "z", 0),
+    ("load", "u", 0),
+    ("load", "z", 1),
+    ("load", "u", 1),
+    ("load", "z", 2),
+    ("load", "z", 3),
+    ("load", "a", 1),
+    ("load", "q", 0),
+    ("load", "k", 0),
+    ("load", "u", 3),
+    ("load", "d", 0),
+    ("load", "u", 2),
+    ("setup",),
+    ("t_z", 0, 0, 5),
+    ("il_a", "s", 0),
+    ("il_a", "g", 1),
+    ("il_u", "v", 0),
+    ("g_q",),
+    ("t_z", 0, 1, 7),
+    ("e_z", 0, 0, "s"),
+    ("e_z", 0, 1, "s"),
+    ("t_z", 1, 0, 4),
+    ("q_a", 0),
+    ("q_z", 0, 0, 1),
+    ("q_u", 0, 1),
+    ("il_u", "v", 1),
+    ("e_z", 1, 0, "s"),
+    ("t_z", 1, 1, 5),
+    ("q_z", 0, 1, 1),
+    ("q_u", 1, 1),
+    ("m_s", 0, 0, 0, 2),
+    ("e_s", 0, 0, 0),
+    ("m_pay", 1, 0, 6),
+    ("e_z", 1, 1, "s"),
+    ("q_z", 1, 1, 1),
+    ("m_pay", 0, 0, 7),
+    ("t_d", 4),
+    ("e_pay", 0, 0),
+    ("q_z", 1, 0, 1),
+    ("m_s", 0, 0, 3, 2),
+    ("m_s", 0, 0, 1, 3),
+    ("q_a", 1),
+    ("e_s", 0, 0, 3),
+    ("e_pay", 1, 0),
+    ("m_pay", 1, 1, 1),
+    ("e_s", 0, 0, 1),
+    ("il_u", "g", 2, 0),
+    ("m_s", 0, 0, 2, 6),
+    ("m_pay", 0, 1, 2),
+    ("m_s", 1, 0, 0, 5),
+    ("il_u", "g", 2, 1),
+    ("e_pay", 1, 1),
+    ("e_pay", 0, 1),
+    ("m_pay", 3, 1, 7),
+    ("m_s", 1, 0, 1, 1),
+    ("m_pay", 2, 1, 0),
+    ("e_pay", 3, 1),
+    ("e_s", 0, 0, 2),
+    ("il_u", "g", 3, 1),
+    ("m_pay", 2, 0, 6),
+    ("e_s", 1, 0, 0),
+    ("g_mean", 0),
+    ("e_s", 1, 0, 1),
+    ("g_mean", 1),
+    ("m_s", 1, 0, 3, 2),
+    ("e_pay", 2, 1),
+    ("il_u", "g", 3, 0),
+    ("m_pay", 3, 0, 7),
+    ("v_b", 0),
+    ("e_pay", 2, 0),
+    ("q_u", 2, 1),
+    ("e_pay", 3, 0),
+    ("t_b", 0, 6),
+    ("q_u", 3, 1),
+    ("m_s", 1, 0, 2, 5),
+    ("e_s", 1, 0, 3),
+    ("e_b", 0, "s"),
+    ("m_r", 0, 1, 2, 3),
+    ("v_b", 1),
+    ("m_r", 0, 1, 0, 2),
+    ("g_mean", 3),
+    ("e_r", 0, 1, 2),
+    ("q_s", 0, 0),
+    ("e_s", 1, 0, 2),
+    ("g_mean", 2),
+    ("m_r", 0, 1, 1, 6),
+    ("m_s", 1, 1, 3, 7),
+    ("t_b", 1, 0),
+    ("e_r", 0, 1, 1),
+    ("m_s", 1, 1, 1, 6),
+    ("e_b", 1, "s"),
+    ("m_r", 0, 1, 3, 1),
+    ("q_b", 0),
+    ("q_s", 1, 0),
+    ("e_r", 0, 1, 0),
+    ("e_r", 0, 1, 3),
+    ("m_s", 1, 1, 2, 3),
+    ("q_b", 1),
+    ("m_t0", 0, 0, 0),
+    ("il_s", "g", 0, 1, 2),
+    ("m_o0", 0, 0, 5),
+    ("m_t1", 0, 0),
+    ("v_b", 2),
+    ("m_s", 1, 1, 0, 2),
+    ("v_b", 3),
+    ("e_t", 0, 0, "s"),
+    ("m_o1", 0, 0),
+    ("e_s", 1, 1, 3),
+    ("e_o", 0, 0, "s"),
+    ("m_o0", 1, 0, 1),
+    ("t_b", 2, 0),
+    ("m_t0", 1, 0, 5),
+    ("il_s", "g", 0, 1, 3),
+    ("e_b", 2, "s"),
+    ("q_b", 2),
+    ("e_s", 1, 1, 2),
+    ("t_b", 3, 4),
+    ("il_s", "g", 0, 1, 0),
+    ("e_b", 3, "s"),
+    ("m_o1", 1, 0),
+    ("m_t1", 1, 0),
+    ("m_o0", 2, 0, 0),
+    ("e_o", 1, 0, "s"),
+    ("q_b", 3),
+    ("il_s", "g", 0, 1, 1),
+    ("e_t", 1, 0, "s"),
+    ("m_o1", 2, 0),
+    ("e_s", 1, 1, 1),
+    ("m_t0", 2, 0, 7),
+    ("m_t1", 2, 0),
+    ("m_t0", 3, 0, 1),
+    ("m_o0", 3, 0, 6),
+    ("q_s", 0, 1),
+    ("m_t1", 3, 0),
+    ("m_o1", 3, 0),
+    ("e_s", 1, 1, 0),
+    ("m_t0", 1, 1, 4),
+    ("e_o", 2, 0, "s"),
+    ("e_t", 2, 0, "s"),
+    ("m_o0", 1, 1, 3),
+    ("m_t0", 0, 1, 0),
+    ("e_o", 3, 0, "s"),
+    ("q_o", 0, 0),
+    ("e_t", 3, 0, "s"),
+    ("q_s", 1, 1),
+    ("q_o", 2, 0),
+    ("m_o0", 2, 1, 5),
+    ("m_o1", 2, 1),
+    ("st_o", 1, 0),
+    ("m_o1", 1, 1),
+    ("m_t0", 2, 1, 1),
+    ("m_t1", 2, 1),
+    ("m_t1", 1, 1),
+    ("m_t1", 0, 1),
+    ("e_o", 1, 1, "s"),
+    ("st_o", 2, 0),
+    ("st_o", 3, 0),
+    ("q_o", 1, 0),
+    ("q_o", 3, 0),
+    ("m_o0", 3, 1, 6),
+    ("st_o", 0, 0),
+    ("m_o1", 3, 1),
+    ("e_t", 1, 1, "s"),
+    ("m_o0", 0, 1, 2),
+    ("e_o", 2, 1, "v"),
+    ("m_o1", 0, 1),
+    ("e_o", 3, 1, "s"),
+    ("e_t", 2, 1, "v"),
+    ("e_o", 0, 1, "s"),
+    ("st_w", 0, 0, 4),
+    ("st_o", 1, 1),
+    ("e_t", 0, 1, "v"),
+    ("m_t0", 3, 1, 3),
+    ("m_t1", 3, 1),
+    ("q_o", 2, 1),
+    ("q_o", 1, 1),
+    ("st_o", 2, 1),
+    ("st_o", 3, 1),
+    ("e_t", 3, 1, "s"),
+    ("q_o", 0, 1),
+    ("st_o", 0, 1),
+    ("st_w", 1, 0, 2),
+    ("q_o", 3, 1),
+    ("st_w", 1, 2, 4),
+    ("st_s", 3),
+    ("st_s", 2),
+    ("st_s", 1),
+    ("st_s", 0),
+]
+
+
+def tile_likelihoodratiobachelierbasketdeltas_x1_kernel(tc, z, a, k, d, u, q, out_0, out_1, out_2):
+    nc = tc.nc
+    with ExitStack() as ctx:
+        sb = ctx.enter_context(tc.tile_pool(name="sb", bufs=1))
+        ps = ctx.enter_context(tc.psum_pool(name="ps", bufs=1))
+        ctx.enter_context(tc.manual_schedule())
+
+        def tile(name, shape, dtype):
+            return sb.tile(shape, dtype, name=name, align_bytes=256)
+
+        ident = tile("ident", [128, 128], F32)
+        warm = tile("warm", [128, 8], F32)
+        z_raw = tile("z_raw", [128, 2, 4, K], BF16)
+        u_raw = [tile("u_raw%d" % i, [128, 4, 256], BF16) for i in range(4)]
+        a_raw = [tile("a_raw%d" % i, [128, 4, 256], BF16) for i in range(2)]
+        s_raw = tile("s_raw", [128, 2, 2, 4, 512], BF16)
+        q_f32 = tile("q_f32", [128, 2, 4], F32)
+        q_sb = tile("q_sb", [128, 2, 4], BF16)
+        d_sb = tile("d_sb", [128, 2, 4], BF16)
+        k_sb = tile("k_sb", [128, 4, 2], BF16)
+        z_grp = tile("z_grp", [128, 2, 2048], BF16)
+        u_grp = tile("u_grp", [128, 4096], BF16)
+        a_grp = tile("a_grp", [128, 2048], BF16)
+        z_code = tile("z_code", [128, 2, 512], U32)
+        z_scale = tile("z_scale", [128, 2, 512], U8)
+        u_code = tile("u_code", [128, 1024], U32)
+        u_scale = tile("u_scale", [128, 1024], U8)
+        a_code = tile("a_code", [128, 512], U32)
+        a_scale = tile("a_scale", [128, 512], U8)
+        pay = tile("pay", [128, 4, 1024], F32)
+        sums = tile("sums", [128, 4, 2], F32)
+        mean = [tile("mean%d" % j, [128, 1], F32) for j in range(4)]
+        bt = tile("bt", [128, 4, 1024], BF16)
+        b_grp = tile("b_grp", [128, 4, 1024], BF16)
+        b_code = tile("b_code", [128, 4, 256], U32)
+        b_scale = tile("b_scale", [128, 4, 256], U8)
+        s_grp = tile("s_grp", [128, 2, 2, 2048], BF16)
+        s_code = tile("s_code", [128, 2, 2, 512], U32)
+        s_scale = tile("s_scale", [128, 2, 2, 512], U8)
+        o_f32 = tile("o_f32", [128, 4, 2, 512], F32)
+        o_grp = tile("o_grp", [128, 2, 4, 512], BF16)
+        o_code = tile("o_code", [128, 2, 512], U32)
+        o_scale = tile("o_scale", [128, 2, 512], U8)
+
+        banks = {}
+
+        def bank(key, index):
+            banks[key] = ps.tile([128, 512], F32, name="bank", tag="bank%d" % index)
+            return banks[key]
+
+        def quantize(code, scale, grp):
+            nc.vector.quantize_mx(out=code.bitcast(FP8X4), scales=scale, in_=grp)
+
+        def mx(out, lc, ls, rc, rs, start, stop):
+            nc.tensor.matmul_mx(out=out, lhsT=lc.bitcast(FP8X4), lhsT_scale=ls, rhs=rc.bitcast(FP8X4), rhs_scale=rs,
+                                start=start, stop=stop)
+
+        def copy(engine, dst, src):
+            if engine == "v":
+                nc.vector.tensor_copy(out=dst, in_=src)
+            else:
+                nc.scalar.copy(out=dst, in_=src)
+
+        def m_t_pass(j, h, g, b):
+            c = slice(128 * g, 128 * (g + 1))
+            for r in range(4):
+                n = slice(128 * r, 128 * (r + 1))
+                mx(b[:, n], s_code[:, h, g, n], s_scale[:, h, g, n], b_code[:, j, c], b_scale[:, j, c],
+                   g == 0 and r == 0, g == 1 and r == 3)
+
+        def m_t0(j, h, index):
+            m_t_pass(j, h, 0, bank(("t", j, h), index))
+
+        def m_t1(j, h):
+            m_t_pass(j, h, 1, banks[("t", j, h)])
+
+        def m_r(g, h, t, index):
+            b = bank(("r", g, h, t), index)
+            m = slice(128 * t, 128 * (t + 1))
+            n = slice(512 * h, 512 * (h + 1))
+            mx(b[:], z_code[:, g, m], z_scale[:, g, m], u_code[:, n], u_scale[:, n], True, True)
+
+        def e_r(g, h, t):
+            nc.scalar.activation(out=s_raw[:, h, g, t, :].rearrange("p (r n) -> p r n", r=4),
+                                 in_=banks[("r", g, h, t)][:].rearrange("p (n r) -> p r n", r=4),
+                                 func=ACT.Copy, scale=q_f32[:, g, t : t + 1])
+
+        def il_s(engine, g, h, c):
+            interleave(engine, s_grp[:, h, g, 512 * c : 512 * (c + 1)], s_raw[:, h, g, :, 128 * c : 128 * (c + 1)])
+
+        def g_q():
+            nc.gpsimd.tensor_copy(out=q_f32[:], in_=q_sb[:])
+
+        def load(name, i):
+            if name == "z":
+                g, half = divmod(i, 2)
+                src = z[512 * g : 512 * (g + 1), :].rearrange("(p t) k -> p t k", t=4)
+                nc.sync.dma_start(out=z_raw[:, g, 2 * half : 2 * half + 2, :], in_=src[:, 2 * half : 2 * half + 2, :])
+            if name == "u":
+                src = u.rearrange("(p j) n -> p j n", j=4)
+                nc.sync.dma_start(out=u_raw[i][:], in_=src[:, :, 256 * i : 256 * (i + 1)])
+            if name == "a":
+                src = a.rearrange("(p j) c -> p j c", j=4)
+                nc.sync.dma_start(out=a_raw[i][:], in_=src[:, :, 256 * i : 256 * (i + 1)])
+            if name == "q":
+                nc.sync.dma_start(out=q_sb[:], in_=q.rearrange("(g p t) -> p g t", g=2, t=4))
+            if name == "d":
+                nc.sync.dma_start(out=d_sb[:], in_=d.rearrange("(g p t) -> p g t", g=2, t=4))
+            if name == "k":
+                with nc.allow_non_contiguous_dma(reason="one offset for each partition and basket tile"):
+                    nc.sync.dma_start(out=k_sb[:, :, 0], in_=k.rearrange("(j c) -> c j", j=4))
+
+        def interleave(engine, dst, src):
+            if engine == "g":
+                nc.gpsimd.tensor_scalar(out=dst.rearrange("p (c t) -> p c t", t=4), in0=src.rearrange("p t c -> p c t"),
+                                        scalar1=1.0, scalar2=0.0, op0=ALU.mult, op1=ALU.add)
+                return
+            o = dst.rearrange("p (c i t) -> p c t i", i=4, t=4)
+            s = src.rearrange("p t (c i) -> p c t i", i=4)
+            if engine == "v":
+                nc.vector.tensor_copy(out=o, in_=s)
+            else:
+                nc.scalar.copy(out=o, in_=s)
+
+        def il_u(engine, i, part=None):
+            if part is None:
+                interleave(engine, u_grp[:, 1024 * i : 1024 * (i + 1)], u_raw[i][:])
+            else:
+                lo = 1024 * i + 512 * part
+                interleave(engine, u_grp[:, lo : lo + 512], u_raw[i][:, :, 128 * part : 128 * (part + 1)])
+
+        def q_u(i, count):
+            quantize(u_code[:, 256 * i : 256 * (i + count)], u_scale[:, 256 * i : 256 * (i + count)],
+                     u_grp[:, 1024 * i : 1024 * (i + count)])
+
+        def il_a(engine, i):
+            interleave(engine, a_grp[:, 1024 * i : 1024 * (i + 1)], a_raw[i][:])
+
+        def q_a(i):
+            quantize(a_code[:, 256 * i : 256 * (i + 1)], a_scale[:, 256 * i : 256 * (i + 1)],
+                     a_grp[:, 1024 * i : 1024 * (i + 1)])
+
+        def t_z(g, half, index):
+            b = bank(("z", g, half), index)
+            for t in (2 * half, 2 * half + 1):
+                words = z_raw[:, g, t, :].bitcast(F32)
+                for w in range(2):
+                    col = 256 * (t - 2 * half) + 128 * w
+                    nc.tensor.transpose(b[:, col : col + 128], words[:, w : 256 : 2], ident[:])
+
+        def e_z(g, half, engine):
+            dst = z_grp[:, g, 1024 * half : 1024 * (half + 1)].bitcast(F32).rearrange("p (t m w) -> p t m w", t=2, w=2)
+            copy(engine, dst, banks[("z", g, half)][:].rearrange("p (t w m) -> p t m w", t=2, w=2))
+
+        def q_z(g, half, count):
+            lo, hi = 256 * half, 256 * (half + count)
+            quantize(z_code[:, g, lo:hi], z_scale[:, g, lo:hi], z_grp[:, g, 4 * lo : 4 * hi])
+
+        def m_s(g, h, c, index):
+            b = bank(("s", g, h, c), index)
+            n = slice(512 * h + 128 * c, 512 * h + 128 * (c + 1))
+            for t in range(4):
+                m = slice(128 * t, 128 * (t + 1))
+                mx(b[:, m], z_code[:, g, m], z_scale[:, g, m], u_code[:, n], u_scale[:, n], True, True)
+
+        def e_s(g, h, c):
+            dst = s_grp[:, h, g, :].rearrange("p (r n t) -> p r n t", r=4, t=4)[:, :, 32 * c : 32 * (c + 1), :]
+            src = banks[("s", g, h, c)][:].rearrange("p (t n r) -> p r n t", t=4, r=4)
+            fac = q_sb[:, g, :].unsqueeze(1).unsqueeze(1).to_broadcast([128, 4, 32, 4])
+            nc.vector.tensor_tensor(out=dst, in0=src, in1=fac, op=ALU.mult)
+
+        def q_s(g, h):
+            quantize(s_code[:, h, g, :], s_scale[:, h, g, :], s_grp[:, h, g, :])
+
+        def m_pay(j, g, index):
+            b = bank(("pay", j, g), index)
+            c = slice(128 * j, 128 * (j + 1))
+            mx(b[:], a_code[:, c], a_scale[:, c], z_code[:, g, :], z_scale[:, g, :], True, True)
+
+        def e_pay(j, g):
+            dst = pay[:, j, 512 * g : 512 * (g + 1)].rearrange("p (w m e) -> p w m e", w=2, e=2)
+            src = banks[("pay", j, g)][:].rearrange("p (w e m) -> p w m e", w=2, e=2)
+            nc.scalar.activation(out=dst, in_=src, func=ACT.Relu, bias=k_sb[:, j, 0:1], accum_out=sums[:, j, g : g + 1])
+
+        def g_mean(j):
+            nc.gpsimd.tensor_scalar(out=mean[j][:], in0=sums[:, j, 0:1], scalar1=sums[:, j, 1:2], scalar2=1.0 / M,
+                                    op0=ALU.add, op1=ALU.mult)
+
+        def t_d(index):
+            b = bank("d", index)
+            words = d_sb[:].rearrange("p g t -> p (g t)").bitcast(F32)
+            for i in range(4):
+                nc.tensor.transpose(b[:, 128 * i : 128 * (i + 1)], words[:, i : i + 1].to_broadcast([128, 128]), ident[:])
+
+        def v_b(j):
+            nc.vector.scalar_tensor_tensor(out=bt[:, j, :], in0=pay[:, j, :], scalar=mean[j][:],
+                                           in1=banks["d"][:].bitcast(BF16), op0=ALU.subtract, op1=ALU.mult)
+
+        def t_b(j, index):
+            b = bank(("b", j), index)
+            words = bt[:, j, :].bitcast(F32)
+            for i in range(4):
+                nc.tensor.transpose(b[:, 128 * i : 128 * (i + 1)], words[:, 128 * i : 128 * (i + 1)], ident[:])
+
+        def e_b(j, engine):
+            dst = b_grp[:, j, :].bitcast(F32).rearrange("p (g c w) -> p g c w", g=2, w=2)
+            copy(engine, dst, banks[("b", j)][:].rearrange("p (g w c) -> p g c w", g=2, w=2))
+
+        def q_b(j):
+            quantize(b_code[:, j, :], b_scale[:, j, :], b_grp[:, j, :])
+
+        def m_o0(j, h, tag):
+            b = bank(("o", j, h), tag)
+            mx(b[:], b_code[:, j, 0:128], b_scale[:, j, 0:128], s_code[:, h, 0, :], s_scale[:, h, 0, :], True, False)
+
+        def m_o1(j, h):
+            b = banks[("o", j, h)]
+            mx(b[:], b_code[:, j, 128:256], b_scale[:, j, 128:256], s_code[:, h, 1, :], s_scale[:, h, 1, :], False, True)
+
+        def scaled_copy(engine, dst, src):
+            if engine == "v":
+                nc.vector.tensor_scalar(out=dst, in0=src, scalar1=1.0 / 32, scalar2=None, op0=ALU.mult)
+            else:
+                nc.scalar.activation(out=dst, in_=src, func=ACT.Copy, scale=1.0 / 32)
+
+        def e_o(j, h, engine):
+            scaled_copy(engine, o_f32[:, j, h, :].rearrange("p (n r) -> p n r", r=4),
+                        banks[("o", j, h)][:].rearrange("p (r n) -> p n r", r=4))
+
+        def e_t(j, h, engine):
+            scaled_copy(engine, o_grp[:, h, j, :].rearrange("p (c r) -> p c r", r=4),
+                        banks[("t", j, h)][:].rearrange("p (r c) -> p c r", r=4))
+
+        def q_o(j, h):
+            c = slice(128 * j, 128 * (j + 1))
+            quantize(o_code[:, h, c], o_scale[:, h, c], o_grp[:, h, j, :])
+
+        def st_o(j, h):
+            nc.sync.dma_start(out=out_0[128 * j : 128 * (j + 1), 512 * h : 512 * (h + 1)], in_=o_f32[:, j, h, :])
+
+        def st_w(h, j0, j1):
+            dst = out_1[h].rearrange("p m t -> p (m t)").bitcast(I32)
+            nc.sync.dma_start(out=dst[:, 128 * j0 : 128 * j1], in_=o_code[:, h, 128 * j0 : 128 * j1].bitcast(I32))
+
+        def st_s(quad):
+            dst = out_2[:, 4 * quad : 4 * quad + 4, :].rearrange("g r m -> r g m").bitcast(I32)
+            eng = nc.sync if quad % 2 == 0 else nc.scalar
+            eng.dma_start(out=dst, in_=o_scale[32 * quad : 32 * quad + 4, :, :].bitcast(I32))
+
+        def setup():
+            make_identity(nc, ident[:])
+            nc.scalar.activation(out=warm[:], in_=ident[:, 0:8], func=ACT.Relu)
+
+        steps = {"load": load, "il_u": il_u, "q_u": q_u, "il_a": il_a, "q_a": q_a, "t_z": t_z, "e_z": e_z, "q_z": q_z, "m_s": m_s, "e_s": e_s, "q_s": q_s, "m_pay": m_pay, "e_pay": e_pay, "g_mean": g_mean, "t_d": t_d, "v_b": v_b, "t_b": t_b, "e_b": e_b, "q_b": q_b, "m_o0": m_o0, "m_o1": m_o1, "m_t0": m_t0, "m_t1": m_t1, "m_r": m_r, "e_r": e_r, "il_s": il_s, "g_q": g_q, "e_o": e_o, "e_t": e_t, "q_o": q_o, "st_o": st_o, "st_w": st_w, "st_s": st_s, "setup": setup}
+        for step in ORDER:
+            steps[step[0]](*step[1:])

@@ -5,6 +5,13 @@ from concourse.masks import make_identity
 
 M, K, P, N = 1024, 512, 512, 1024
 FLOPS = 2 * M * K * (P + N) + 2 * P * M * N
+OUT_SCALE = 1.0 / 32
+
+PART = 128
+SLOTS = 4
+PASS = PART * SLOTS
+BANKS = 8
+PIECE = 256
 
 F32 = mybir.dt.float32
 BF16 = mybir.dt.bfloat16
@@ -15,197 +22,9 @@ FP8X4 = mybir.dt.float8_e4m3fn_x4
 ALU = mybir.AluOpType
 ACT = mybir.ActivationFunctionType
 
-ORDER = [
-    ("load", "a", 0),
-    ("load", "z", 0),
-    ("load", "u", 0),
-    ("load", "z", 1),
-    ("load", "u", 1),
-    ("load", "z", 2),
-    ("load", "z", 3),
-    ("load", "a", 1),
-    ("load", "q", 0),
-    ("load", "k", 0),
-    ("load", "u", 3),
-    ("load", "d", 0),
-    ("load", "u", 2),
-    ("setup",),
-    ("t_z", 0, 0, 5),
-    ("il_a", "s", 0),
-    ("il_a", "g", 1),
-    ("il_u", "v", 0),
-    ("g_q",),
-    ("t_z", 0, 1, 7),
-    ("e_z", 0, 0, "s"),
-    ("e_z", 0, 1, "s"),
-    ("t_z", 1, 0, 4),
-    ("q_a", 0),
-    ("q_z", 0, 0, 1),
-    ("q_u", 0, 1),
-    ("il_u", "v", 1),
-    ("e_z", 1, 0, "s"),
-    ("t_z", 1, 1, 5),
-    ("q_z", 0, 1, 1),
-    ("q_u", 1, 1),
-    ("m_s", 0, 0, 0, 2),
-    ("e_s", 0, 0, 0),
-    ("m_pay", 1, 0, 6),
-    ("e_z", 1, 1, "s"),
-    ("q_z", 1, 1, 1),
-    ("m_pay", 0, 0, 7),
-    ("t_d", 4),
-    ("e_pay", 0, 0),
-    ("q_z", 1, 0, 1),
-    ("m_s", 0, 0, 3, 2),
-    ("m_s", 0, 0, 1, 3),
-    ("q_a", 1),
-    ("e_s", 0, 0, 3),
-    ("e_pay", 1, 0),
-    ("m_pay", 1, 1, 1),
-    ("e_s", 0, 0, 1),
-    ("il_u", "g", 2, 0),
-    ("m_s", 0, 0, 2, 6),
-    ("m_pay", 0, 1, 2),
-    ("m_s", 1, 0, 0, 5),
-    ("il_u", "g", 2, 1),
-    ("e_pay", 1, 1),
-    ("e_pay", 0, 1),
-    ("m_pay", 3, 1, 7),
-    ("m_s", 1, 0, 1, 1),
-    ("m_pay", 2, 1, 0),
-    ("e_pay", 3, 1),
-    ("e_s", 0, 0, 2),
-    ("il_u", "g", 3, 1),
-    ("m_pay", 2, 0, 6),
-    ("e_s", 1, 0, 0),
-    ("g_mean", 0),
-    ("e_s", 1, 0, 1),
-    ("g_mean", 1),
-    ("m_s", 1, 0, 3, 2),
-    ("e_pay", 2, 1),
-    ("il_u", "g", 3, 0),
-    ("m_pay", 3, 0, 7),
-    ("v_b", 0),
-    ("e_pay", 2, 0),
-    ("q_u", 2, 1),
-    ("e_pay", 3, 0),
-    ("t_b", 0, 6),
-    ("q_u", 3, 1),
-    ("m_s", 1, 0, 2, 5),
-    ("e_s", 1, 0, 3),
-    ("e_b", 0, "s"),
-    ("m_r", 0, 1, 2, 3),
-    ("v_b", 1),
-    ("m_r", 0, 1, 0, 2),
-    ("g_mean", 3),
-    ("e_r", 0, 1, 2),
-    ("q_s", 0, 0),
-    ("e_s", 1, 0, 2),
-    ("g_mean", 2),
-    ("m_r", 0, 1, 1, 6),
-    ("m_s", 1, 1, 3, 7),
-    ("t_b", 1, 0),
-    ("e_r", 0, 1, 1),
-    ("m_s", 1, 1, 1, 6),
-    ("e_b", 1, "s"),
-    ("m_r", 0, 1, 3, 1),
-    ("q_b", 0),
-    ("q_s", 1, 0),
-    ("e_r", 0, 1, 0),
-    ("e_r", 0, 1, 3),
-    ("m_s", 1, 1, 2, 3),
-    ("q_b", 1),
-    ("m_t0", 0, 0, 0),
-    ("il_s", "g", 0, 1, 2),
-    ("m_o0", 0, 0, 5),
-    ("m_t1", 0, 0),
-    ("v_b", 2),
-    ("m_s", 1, 1, 0, 2),
-    ("v_b", 3),
-    ("e_t", 0, 0, "s"),
-    ("m_o1", 0, 0),
-    ("e_s", 1, 1, 3),
-    ("e_o", 0, 0, "s"),
-    ("m_o0", 1, 0, 1),
-    ("t_b", 2, 0),
-    ("m_t0", 1, 0, 5),
-    ("il_s", "g", 0, 1, 3),
-    ("e_b", 2, "s"),
-    ("q_b", 2),
-    ("e_s", 1, 1, 2),
-    ("t_b", 3, 4),
-    ("il_s", "g", 0, 1, 0),
-    ("e_b", 3, "s"),
-    ("m_o1", 1, 0),
-    ("m_t1", 1, 0),
-    ("m_o0", 2, 0, 0),
-    ("e_o", 1, 0, "s"),
-    ("q_b", 3),
-    ("il_s", "g", 0, 1, 1),
-    ("e_t", 1, 0, "s"),
-    ("m_o1", 2, 0),
-    ("e_s", 1, 1, 1),
-    ("m_t0", 2, 0, 7),
-    ("m_t1", 2, 0),
-    ("m_t0", 3, 0, 1),
-    ("m_o0", 3, 0, 6),
-    ("q_s", 0, 1),
-    ("m_t1", 3, 0),
-    ("m_o1", 3, 0),
-    ("e_s", 1, 1, 0),
-    ("m_t0", 1, 1, 4),
-    ("e_o", 2, 0, "s"),
-    ("e_t", 2, 0, "s"),
-    ("m_o0", 1, 1, 3),
-    ("m_t0", 0, 1, 0),
-    ("e_o", 3, 0, "s"),
-    ("q_o", 0, 0),
-    ("e_t", 3, 0, "s"),
-    ("q_s", 1, 1),
-    ("q_o", 2, 0),
-    ("m_o0", 2, 1, 5),
-    ("m_o1", 2, 1),
-    ("st_o", 1, 0),
-    ("m_o1", 1, 1),
-    ("m_t0", 2, 1, 1),
-    ("m_t1", 2, 1),
-    ("m_t1", 1, 1),
-    ("m_t1", 0, 1),
-    ("e_o", 1, 1, "s"),
-    ("st_o", 2, 0),
-    ("st_o", 3, 0),
-    ("q_o", 1, 0),
-    ("q_o", 3, 0),
-    ("m_o0", 3, 1, 6),
-    ("st_o", 0, 0),
-    ("m_o1", 3, 1),
-    ("e_t", 1, 1, "s"),
-    ("m_o0", 0, 1, 2),
-    ("e_o", 2, 1, "v"),
-    ("m_o1", 0, 1),
-    ("e_o", 3, 1, "s"),
-    ("e_t", 2, 1, "v"),
-    ("e_o", 0, 1, "s"),
-    ("st_w", 0, 0, 4),
-    ("st_o", 1, 1),
-    ("e_t", 0, 1, "v"),
-    ("m_t0", 3, 1, 3),
-    ("m_t1", 3, 1),
-    ("q_o", 2, 1),
-    ("q_o", 1, 1),
-    ("st_o", 2, 1),
-    ("st_o", 3, 1),
-    ("e_t", 3, 1, "s"),
-    ("q_o", 0, 1),
-    ("st_o", 0, 1),
-    ("st_w", 1, 0, 2),
-    ("q_o", 3, 1),
-    ("st_w", 1, 2, 4),
-    ("st_s", 3),
-    ("st_s", 2),
-    ("st_s", 1),
-    ("st_s", 0),
-]
+
+def cols(i, width, count=1):
+    return slice(width * i, width * (i + count))
 
 
 def tile_likelihoodratiobachelierbasketdeltas_x1_kernel(tc, z, a, k, d, u, q, out_0, out_1, out_2):
@@ -218,249 +37,366 @@ def tile_likelihoodratiobachelierbasketdeltas_x1_kernel(tc, z, a, k, d, u, q, ou
         def tile(name, shape, dtype):
             return sb.tile(shape, dtype, name=name, align_bytes=256)
 
-        ident = tile("ident", [128, 128], F32)
-        warm = tile("warm", [128, 8], F32)
-        z_raw = tile("z_raw", [128, 2, 4, K], BF16)
-        u_raw = [tile("u_raw%d" % i, [128, 4, 256], BF16) for i in range(4)]
-        a_raw = [tile("a_raw%d" % i, [128, 4, 256], BF16) for i in range(2)]
-        s_raw = tile("s_raw", [128, 2, 2, 4, 512], BF16)
-        q_f32 = tile("q_f32", [128, 2, 4], F32)
-        q_sb = tile("q_sb", [128, 2, 4], BF16)
-        d_sb = tile("d_sb", [128, 2, 4], BF16)
-        k_sb = tile("k_sb", [128, 4, 2], BF16)
-        z_grp = tile("z_grp", [128, 2, 2048], BF16)
-        u_grp = tile("u_grp", [128, 4096], BF16)
-        a_grp = tile("a_grp", [128, 2048], BF16)
-        z_code = tile("z_code", [128, 2, 512], U32)
-        z_scale = tile("z_scale", [128, 2, 512], U8)
-        u_code = tile("u_code", [128, 1024], U32)
-        u_scale = tile("u_scale", [128, 1024], U8)
-        a_code = tile("a_code", [128, 512], U32)
-        a_scale = tile("a_scale", [128, 512], U8)
-        pay = tile("pay", [128, 4, 1024], F32)
-        sums = tile("sums", [128, 4, 2], F32)
-        mean = [tile("mean%d" % j, [128, 1], F32) for j in range(4)]
-        bt = tile("bt", [128, 4, 1024], BF16)
-        b_grp = tile("b_grp", [128, 4, 1024], BF16)
-        b_code = tile("b_code", [128, 4, 256], U32)
-        b_scale = tile("b_scale", [128, 4, 256], U8)
-        s_grp = tile("s_grp", [128, 2, 2, 2048], BF16)
-        s_code = tile("s_code", [128, 2, 2, 512], U32)
-        s_scale = tile("s_scale", [128, 2, 2, 512], U8)
-        o_f32 = tile("o_f32", [128, 4, 2, 512], F32)
-        o_grp = tile("o_grp", [128, 2, 4, 512], BF16)
-        o_code = tile("o_code", [128, 2, 512], U32)
-        o_scale = tile("o_scale", [128, 2, 512], U8)
+        ident = tile("ident", [PART, PART], F32)
+        zeros = tile("zeros", [PART, PASS], BF16)
+        z_raw = tile("z_raw", [PART, 2, SLOTS, K], BF16)
+        u_raw = [tile("u_raw%d" % h, [PART, SLOTS, PASS], BF16) for h in range(2)]
+        a_raw = tile("a_raw", [PART, SLOTS, P], BF16)
+        rows = tile("rows", [PART, PASS], BF16)
+        rows_f32 = tile("rows_f32", [PART, PART], F32)
+        vec = tile("vec", [PART, 8, 4], F32)
+        q_f32 = tile("q_f32", [PART, 2, SLOTS], F32)
+        z_int = tile("z_int", [PART, 2, SLOTS * PASS], BF16)
+        u_int = tile("u_int", [PART, SLOTS * N], BF16)
+        a_int = tile("a_int", [PART, SLOTS * P], BF16)
+        z_code = tile("z_code", [PART, 2, PASS], U32)
+        z_scale = tile("z_scale", [PART, 2, PASS], U8)
+        u_code = tile("u_code", [PART, N], U32)
+        u_scale = tile("u_scale", [PART, N], U8)
+        a_code = tile("a_code", [PART, P], U32)
+        a_scale = tile("a_scale", [PART, P], U8)
+        pay = tile("pay", [PART, 4, M], F32)
+        sums = tile("sums", [PART, 4, 2], F32)
+        mean = [tile("mean%d" % j, [PART, 1], F32) for j in range(4)]
+        b_rows = tile("b_rows", [PART, 4, M], BF16)
+        b_int = tile("b_int", [PART, 4, 2 * SLOTS * PART], BF16)
+        b_code = tile("b_code", [PART, 4, 2 * PART], U32)
+        b_scale = tile("b_scale", [PART, 4, 2 * PART], U8)
+        s_slots = tile("s_slots", [PART, 2, SLOTS, PASS], BF16)
+        s_int = tile("s_int", [PART, 2, 2, SLOTS * PASS], BF16)
+        s_code = tile("s_code", [PART, 2, 2, PASS], U32)
+        s_scale = tile("s_scale", [PART, 2, 2, PASS], U8)
+        o_f32 = tile("o_f32", [PART, 4, 2, PASS], F32)
+        o_int = tile("o_int", [PART, 2, SLOTS * P], BF16)
+        o_code = tile("o_code", [PART, 2, P], U32)
+        o_scale = tile("o_scale", [PART, 2, P], U8)
 
-        banks = {}
+        free = list(range(BANKS))
+        held = {}
 
-        def bank(key, index):
-            banks[key] = ps.tile([128, 512], F32, name="bank", tag="bank%d" % index)
-            return banks[key]
+        def take(key):
+            index = free.pop(0)
+            held[key] = (index, ps.tile([PART, PASS], F32, name="bank", tag="bank%d" % index))
+            return held[key][1]
 
-        def quantize(code, scale, grp):
-            nc.vector.quantize_mx(out=code.bitcast(FP8X4), scales=scale, in_=grp)
+        def give(key):
+            index, bank = held[key]
+            free.append(index)
+            return bank
 
-        def mx(out, lc, ls, rc, rs, start, stop):
-            nc.tensor.matmul_mx(out=out, lhsT=lc.bitcast(FP8X4), lhsT_scale=ls, rhs=rc.bitcast(FP8X4), rhs_scale=rs,
-                                start=start, stop=stop)
+        def quantize(code, scale, interleaved):
+            nc.vector.quantize_mx(out=code.bitcast(FP8X4), scales=scale, in_=interleaved)
 
-        def copy(engine, dst, src):
-            if engine == "v":
-                nc.vector.tensor_copy(out=dst, in_=src)
-            else:
-                nc.scalar.copy(out=dst, in_=src)
-
-        def m_t_pass(j, h, g, b):
-            c = slice(128 * g, 128 * (g + 1))
-            for r in range(4):
-                n = slice(128 * r, 128 * (r + 1))
-                mx(b[:, n], s_code[:, h, g, n], s_scale[:, h, g, n], b_code[:, j, c], b_scale[:, j, c],
-                   g == 0 and r == 0, g == 1 and r == 3)
-
-        def m_t0(j, h, index):
-            m_t_pass(j, h, 0, bank(("t", j, h), index))
-
-        def m_t1(j, h):
-            m_t_pass(j, h, 1, banks[("t", j, h)])
-
-        def m_r(g, h, t, index):
-            b = bank(("r", g, h, t), index)
-            m = slice(128 * t, 128 * (t + 1))
-            n = slice(512 * h, 512 * (h + 1))
-            mx(b[:], z_code[:, g, m], z_scale[:, g, m], u_code[:, n], u_scale[:, n], True, True)
-
-        def e_r(g, h, t):
-            nc.scalar.activation(out=s_raw[:, h, g, t, :].rearrange("p (r n) -> p r n", r=4),
-                                 in_=banks[("r", g, h, t)][:].rearrange("p (n r) -> p r n", r=4),
-                                 func=ACT.Copy, scale=q_f32[:, g, t : t + 1])
-
-        def il_s(engine, g, h, c):
-            interleave(engine, s_grp[:, h, g, 512 * c : 512 * (c + 1)], s_raw[:, h, g, :, 128 * c : 128 * (c + 1)])
-
-        def g_q():
-            nc.gpsimd.tensor_copy(out=q_f32[:], in_=q_sb[:])
-
-        def load(name, i):
-            if name == "z":
-                g, half = divmod(i, 2)
-                src = z[512 * g : 512 * (g + 1), :].rearrange("(p t) k -> p t k", t=4)
-                nc.sync.dma_start(out=z_raw[:, g, 2 * half : 2 * half + 2, :], in_=src[:, 2 * half : 2 * half + 2, :])
-            if name == "u":
-                src = u.rearrange("(p j) n -> p j n", j=4)
-                nc.sync.dma_start(out=u_raw[i][:], in_=src[:, :, 256 * i : 256 * (i + 1)])
-            if name == "a":
-                src = a.rearrange("(p j) c -> p j c", j=4)
-                nc.sync.dma_start(out=a_raw[i][:], in_=src[:, :, 256 * i : 256 * (i + 1)])
-            if name == "q":
-                nc.sync.dma_start(out=q_sb[:], in_=q.rearrange("(g p t) -> p g t", g=2, t=4))
-            if name == "d":
-                nc.sync.dma_start(out=d_sb[:], in_=d.rearrange("(g p t) -> p g t", g=2, t=4))
-            if name == "k":
-                with nc.allow_non_contiguous_dma(reason="one offset for each partition and basket tile"):
-                    nc.sync.dma_start(out=k_sb[:, :, 0], in_=k.rearrange("(j c) -> c j", j=4))
+        def mx(out, lhs_code, lhs_scale, rhs_code, rhs_scale, start, stop):
+            nc.tensor.matmul_mx(out=out, lhsT=lhs_code.bitcast(FP8X4), lhsT_scale=lhs_scale,
+                                rhs=rhs_code.bitcast(FP8X4), rhs_scale=rhs_scale, start=start, stop=stop)
 
         def interleave(engine, dst, src):
-            if engine == "g":
-                nc.gpsimd.tensor_scalar(out=dst.rearrange("p (c t) -> p c t", t=4), in0=src.rearrange("p t c -> p c t"),
+            if engine == "gpsimd":
+                nc.gpsimd.tensor_scalar(out=dst.rearrange("p (c t) -> p c t", t=SLOTS), in0=src.rearrange("p t c -> p c t"),
                                         scalar1=1.0, scalar2=0.0, op0=ALU.mult, op1=ALU.add)
                 return
-            o = dst.rearrange("p (c i t) -> p c t i", i=4, t=4)
-            s = src.rearrange("p t (c i) -> p c t i", i=4)
-            if engine == "v":
-                nc.vector.tensor_copy(out=o, in_=s)
+            dst = dst.rearrange("p (c i t) -> p c t i", i=4, t=SLOTS)
+            src = src.rearrange("p t (c i) -> p c t i", i=4)
+            if engine == "vector":
+                nc.vector.tensor_copy(out=dst, in_=src)
             else:
-                nc.scalar.copy(out=o, in_=s)
+                nc.scalar.activation(out=dst, in_=src, func=ACT.Copy)
 
-        def il_u(engine, i, part=None):
-            if part is None:
-                interleave(engine, u_grp[:, 1024 * i : 1024 * (i + 1)], u_raw[i][:])
-            else:
-                lo = 1024 * i + 512 * part
-                interleave(engine, u_grp[:, lo : lo + 512], u_raw[i][:, :, 128 * part : 128 * (part + 1)])
+        def warm_up(count):
+            bank = take("warm")
+            for i in range(count):
+                nc.tensor.matmul(out=bank[:], lhsT=zeros[:, 0:PART], rhs=zeros[:], start=True, stop=True)
+            give("warm")
 
-        def q_u(i, count):
-            quantize(u_code[:, 256 * i : 256 * (i + count)], u_scale[:, 256 * i : 256 * (i + count)],
-                     u_grp[:, 1024 * i : 1024 * (i + count)])
+        def load_z(g, pair):
+            src = z[cols(g, PASS), :].rearrange("(p t) k -> p t k", t=SLOTS)
+            nc.sync.dma_start(out=z_raw[:, g, cols(pair, 2), :], in_=src[:, cols(pair, 2), :])
 
-        def il_a(engine, i):
-            interleave(engine, a_grp[:, 1024 * i : 1024 * (i + 1)], a_raw[i][:])
-
-        def q_a(i):
-            quantize(a_code[:, 256 * i : 256 * (i + 1)], a_scale[:, 256 * i : 256 * (i + 1)],
-                     a_grp[:, 1024 * i : 1024 * (i + 1)])
-
-        def t_z(g, half, index):
-            b = bank(("z", g, half), index)
-            for t in (2 * half, 2 * half + 1):
-                words = z_raw[:, g, t, :].bitcast(F32)
+        def turn_z(g, pair):
+            bank = take(("z", g, pair))
+            for i in range(2):
+                words = z_raw[:, g, 2 * pair + i, :].bitcast(F32)
                 for w in range(2):
-                    col = 256 * (t - 2 * half) + 128 * w
-                    nc.tensor.transpose(b[:, col : col + 128], words[:, w : 256 : 2], ident[:])
+                    nc.tensor.transpose(bank[:, cols(2 * i + w, PART)], words[:, w : K // 2 : 2], ident[:])
+            dst = z_int[:, g, cols(pair, 2 * PASS)].bitcast(F32).rearrange("p (i m w) -> p i m w", i=2, w=2)
+            nc.scalar.copy(out=dst, in_=give(("z", g, pair))[:].rearrange("p (i w m) -> p i m w", i=2, w=2))
 
-        def e_z(g, half, engine):
-            dst = z_grp[:, g, 1024 * half : 1024 * (half + 1)].bitcast(F32).rearrange("p (t m w) -> p t m w", t=2, w=2)
-            copy(engine, dst, banks[("z", g, half)][:].rearrange("p (t w m) -> p t m w", t=2, w=2))
+        def quantize_z(g):
+            quantize(z_code[:, g, :], z_scale[:, g, :], z_int[:, g, :])
 
-        def q_z(g, half, count):
-            lo, hi = 256 * half, 256 * (half + count)
-            quantize(z_code[:, g, lo:hi], z_scale[:, g, lo:hi], z_grp[:, g, 4 * lo : 4 * hi])
+        def interleave_u(engine, first, width):
+            h, start = divmod(first, PASS)
+            interleave(engine, u_int[:, SLOTS * first : SLOTS * (first + width)], u_raw[h][:, :, start : start + width])
 
-        def m_s(g, h, c, index):
-            b = bank(("s", g, h, c), index)
-            n = slice(512 * h + 128 * c, 512 * h + 128 * (c + 1))
-            for t in range(4):
-                m = slice(128 * t, 128 * (t + 1))
-                mx(b[:, m], z_code[:, g, m], z_scale[:, g, m], u_code[:, n], u_scale[:, n], True, True)
+        def quantize_u(i, count):
+            quantize(u_code[:, cols(i, PIECE, count)], u_scale[:, cols(i, PIECE, count)],
+                     u_int[:, cols(i, SLOTS * PIECE, count)])
 
-        def e_s(g, h, c):
-            dst = s_grp[:, h, g, :].rearrange("p (r n t) -> p r n t", r=4, t=4)[:, :, 32 * c : 32 * (c + 1), :]
-            src = banks[("s", g, h, c)][:].rearrange("p (t n r) -> p r n t", t=4, r=4)
-            fac = q_sb[:, g, :].unsqueeze(1).unsqueeze(1).to_broadcast([128, 4, 32, 4])
-            nc.vector.tensor_tensor(out=dst, in0=src, in1=fac, op=ALU.mult)
+        def turn_vectors():
+            nc.vector.tensor_copy(out=rows_f32[:], in_=rows[:, 0:PART])
+            bank = take("vec")
+            words = rows[:].bitcast(F32)
+            for w in range(2):
+                nc.tensor.transpose(bank[:, cols(w, PART)], words[:, w : PASS // 2 : 2], ident[:])
+            nc.tensor.transpose(bank[:, cols(2, PART)], rows_f32[:], ident[:])
+            src = give("vec")[:, 0 : 3 * PART].rearrange("p (s row) -> p row s", s=3)
+            nc.scalar.copy(out=vec[:, :, 0:3], in_=src[:, 0:8, :])
+            nc.gpsimd.tensor_copy(out=q_f32[:], in_=vec[:, 2:4, :].bitcast(BF16)[:, :, 0:SLOTS])
 
-        def q_s(g, h):
-            quantize(s_code[:, h, g, :], s_scale[:, h, g, :], s_grp[:, h, g, :])
+        def spread_d():
+            bank = take("d")
+            for g in range(2):
+                for w in range(2):
+                    nc.tensor.transpose(bank[:, cols(2 * g + w, PART)],
+                                        vec[:, g, w : w + 1].to_broadcast([PART, PART]), ident[:])
 
-        def m_pay(j, g, index):
-            b = bank(("pay", j, g), index)
-            c = slice(128 * j, 128 * (j + 1))
-            mx(b[:], a_code[:, c], a_scale[:, c], z_code[:, g, :], z_scale[:, g, :], True, True)
+        def multiply_pay(j, g):
+            mx(take(("pay", j, g))[:], a_code[:, cols(j, PART)], a_scale[:, cols(j, PART)],
+               z_code[:, g, :], z_scale[:, g, :], True, True)
 
-        def e_pay(j, g):
-            dst = pay[:, j, 512 * g : 512 * (g + 1)].rearrange("p (w m e) -> p w m e", w=2, e=2)
-            src = banks[("pay", j, g)][:].rearrange("p (w e m) -> p w m e", w=2, e=2)
-            nc.scalar.activation(out=dst, in_=src, func=ACT.Relu, bias=k_sb[:, j, 0:1], accum_out=sums[:, j, g : g + 1])
+        def read_pay(j, g):
+            dst = pay[:, j, cols(g, PASS)].rearrange("p (w m e) -> p w m e", w=2, e=2)
+            src = give(("pay", j, g))[:].rearrange("p (w e m) -> p w m e", w=2, e=2)
+            nc.scalar.activation(out=dst, in_=src, func=ACT.Relu, bias=vec[:, 4 + j, 2:3],
+                                 accum_out=sums[:, j, g : g + 1])
 
-        def g_mean(j):
-            nc.gpsimd.tensor_scalar(out=mean[j][:], in0=sums[:, j, 0:1], scalar1=sums[:, j, 1:2], scalar2=1.0 / M,
+        def mean_pay(j):
+            nc.vector.tensor_scalar(out=mean[j][:], in0=sums[:, j, 0:1], scalar1=sums[:, j, 1:2], scalar2=1.0 / M,
                                     op0=ALU.add, op1=ALU.mult)
 
-        def t_d(index):
-            b = bank("d", index)
-            words = d_sb[:].rearrange("p g t -> p (g t)").bitcast(F32)
+        def make_b(j):
+            nc.vector.scalar_tensor_tensor(out=b_rows[:, j, :], in0=pay[:, j, :], scalar=mean[j][:],
+                                           in1=held["d"][1][:].bitcast(BF16), op0=ALU.subtract, op1=ALU.mult)
+
+        def turn_b(j):
+            bank = take(("b", j))
+            words = b_rows[:, j, :].bitcast(F32)
             for i in range(4):
-                nc.tensor.transpose(b[:, 128 * i : 128 * (i + 1)], words[:, i : i + 1].to_broadcast([128, 128]), ident[:])
+                nc.tensor.transpose(bank[:, cols(i, PART)], words[:, cols(i, PART)], ident[:])
 
-        def v_b(j):
-            nc.vector.scalar_tensor_tensor(out=bt[:, j, :], in0=pay[:, j, :], scalar=mean[j][:],
-                                           in1=banks["d"][:].bitcast(BF16), op0=ALU.subtract, op1=ALU.mult)
+        def read_b(j):
+            dst = b_int[:, j, :].bitcast(F32).rearrange("p (g c w) -> p g c w", g=2, w=2)
+            nc.scalar.copy(out=dst, in_=give(("b", j))[:].rearrange("p (g w c) -> p g c w", g=2, w=2))
 
-        def t_b(j, index):
-            b = bank(("b", j), index)
-            words = bt[:, j, :].bitcast(F32)
-            for i in range(4):
-                nc.tensor.transpose(b[:, 128 * i : 128 * (i + 1)], words[:, 128 * i : 128 * (i + 1)], ident[:])
+        def quantize_b(j):
+            quantize(b_code[:, j, :], b_scale[:, j, :], b_int[:, j, :])
 
-        def e_b(j, engine):
-            dst = b_grp[:, j, :].bitcast(F32).rearrange("p (g c w) -> p g c w", g=2, w=2)
-            copy(engine, dst, banks[("b", j)][:].rearrange("p (g w c) -> p g c w", g=2, w=2))
+        def multiply_s_chunk(h, c):
+            bank = take(("s", h, c))
+            n = cols(4 * h + c, PART)
+            for t in range(SLOTS):
+                m = cols(t, PART)
+                mx(bank[:, m], z_code[:, h, m], z_scale[:, h, m], u_code[:, n], u_scale[:, n], True, True)
 
-        def q_b(j):
-            quantize(b_code[:, j, :], b_scale[:, j, :], b_grp[:, j, :])
+        def read_s_chunk(h, c):
+            dst = s_int[:, h, h, :].rearrange("p (r n t) -> p r n t", r=SLOTS, t=SLOTS)[:, :, cols(c, PART // SLOTS), :]
+            src = give(("s", h, c))[:].rearrange("p (t n r) -> p r n t", t=SLOTS, r=SLOTS)
+            factor = vec[:, 2 + h, 0:2].bitcast(BF16).unsqueeze(1).unsqueeze(1)
+            nc.vector.tensor_tensor(out=dst, in0=src, in1=factor.to_broadcast([PART, SLOTS, PART // SLOTS, SLOTS]),
+                                    op=ALU.mult)
 
-        def m_o0(j, h, tag):
-            b = bank(("o", j, h), tag)
-            mx(b[:], b_code[:, j, 0:128], b_scale[:, j, 0:128], s_code[:, h, 0, :], s_scale[:, h, 0, :], True, False)
+        def multiply_s_slot(h, t):
+            m, n = cols(t, PART), cols(h, PASS)
+            mx(take(("slot", h, t))[:], z_code[:, 1 - h, m], z_scale[:, 1 - h, m], u_code[:, n], u_scale[:, n], True, True)
 
-        def m_o1(j, h):
-            b = banks[("o", j, h)]
-            mx(b[:], b_code[:, j, 128:256], b_scale[:, j, 128:256], s_code[:, h, 1, :], s_scale[:, h, 1, :], False, True)
+        def read_s_slot(h, t):
+            nc.scalar.activation(out=s_slots[:, h, t, :].rearrange("p (r n) -> p r n", r=SLOTS),
+                                 in_=give(("slot", h, t))[:].rearrange("p (n r) -> p r n", r=SLOTS),
+                                 func=ACT.Copy, scale=q_f32[:, 1 - h, t : t + 1])
+
+        def interleave_s(engine, h, i):
+            interleave(engine, s_int[:, h, 1 - h, cols(i, SLOTS * PIECE)], s_slots[:, h, :, cols(i, PIECE)])
+
+        def quantize_s(g, h):
+            quantize(s_code[:, h, g, :], s_scale[:, h, g, :], s_int[:, h, g, :])
+
+        def multiply_out(j, h, g):
+            bank = take(("out", j, h)) if g == 0 else held[("out", j, h)][1]
+            c = cols(g, PART)
+            mx(bank[:], b_code[:, j, c], b_scale[:, j, c], s_code[:, h, g, :], s_scale[:, h, g, :], g == 0, g == 1)
+
+        def multiply_out_t(j, h, g):
+            bank = take(("out_t", j, h)) if g == 0 else held[("out_t", j, h)][1]
+            c = cols(g, PART)
+            for r in range(SLOTS):
+                n = cols(r, PART)
+                mx(bank[:, n], s_code[:, h, g, n], s_scale[:, h, g, n], b_code[:, j, c], b_scale[:, j, c],
+                   g == 0 and r == 0, g == 1 and r == SLOTS - 1)
 
         def scaled_copy(engine, dst, src):
-            if engine == "v":
-                nc.vector.tensor_scalar(out=dst, in0=src, scalar1=1.0 / 32, scalar2=None, op0=ALU.mult)
+            if engine == "vector":
+                nc.vector.tensor_scalar(out=dst, in0=src, scalar1=OUT_SCALE, scalar2=None, op0=ALU.mult)
             else:
-                nc.scalar.activation(out=dst, in_=src, func=ACT.Copy, scale=1.0 / 32)
+                nc.scalar.activation(out=dst, in_=src, func=ACT.Copy, scale=OUT_SCALE)
 
-        def e_o(j, h, engine):
-            scaled_copy(engine, o_f32[:, j, h, :].rearrange("p (n r) -> p n r", r=4),
-                        banks[("o", j, h)][:].rearrange("p (r n) -> p n r", r=4))
+        def store_out(engine, j, h):
+            scaled_copy(engine, o_f32[:, j, h, :].rearrange("p (n r) -> p n r", r=SLOTS),
+                        give(("out", j, h))[:].rearrange("p (r n) -> p n r", r=SLOTS))
+            nc.sync.dma_start(out=out_0[cols(j, PART), cols(h, PASS)], in_=o_f32[:, j, h, :])
 
-        def e_t(j, h, engine):
-            scaled_copy(engine, o_grp[:, h, j, :].rearrange("p (c r) -> p c r", r=4),
-                        banks[("t", j, h)][:].rearrange("p (r c) -> p c r", r=4))
+        def read_out_t(engine, j, h):
+            scaled_copy(engine, o_int[:, h, cols(j, PASS)].rearrange("p (c r) -> p c r", r=SLOTS),
+                        give(("out_t", j, h))[:].rearrange("p (r c) -> p c r", r=SLOTS))
 
-        def q_o(j, h):
-            c = slice(128 * j, 128 * (j + 1))
-            quantize(o_code[:, h, c], o_scale[:, h, c], o_grp[:, h, j, :])
+        def store_codes(h, j, count):
+            c = cols(j, PART, count)
+            quantize(o_code[:, h, c], o_scale[:, h, c], o_int[:, h, cols(j, PASS, count)])
+            dst = out_1[h].rearrange("p m r -> p (m r)").bitcast(I32)
+            nc.sync.dma_start(out=dst[:, c], in_=o_code[:, h, c].bitcast(I32))
 
-        def st_o(j, h):
-            nc.sync.dma_start(out=out_0[128 * j : 128 * (j + 1), 512 * h : 512 * (h + 1)], in_=o_f32[:, j, h, :])
+        def store_scales(quadrant):
+            dst = out_2[:, cols(quadrant, 4), :].rearrange("h row m -> row h m").bitcast(I32)
+            queue = nc.sync if quadrant % 2 == 0 else nc.scalar
+            queue.dma_start(out=dst, in_=o_scale[32 * quadrant : 32 * quadrant + 4, :, :].bitcast(I32))
 
-        def st_w(h, j0, j1):
-            dst = out_1[h].rearrange("p m t -> p (m t)").bitcast(I32)
-            nc.sync.dma_start(out=dst[:, 128 * j0 : 128 * j1], in_=o_code[:, h, 128 * j0 : 128 * j1].bitcast(I32))
 
-        def st_s(quad):
-            dst = out_2[:, 4 * quad : 4 * quad + 4, :].rearrange("g r m -> r g m").bitcast(I32)
-            eng = nc.sync if quad % 2 == 0 else nc.scalar
-            eng.dma_start(out=dst, in_=o_scale[32 * quad : 32 * quad + 4, :, :].bitcast(I32))
+        nc.gpsimd.memset(rows[:].bitcast(I32), 0)
+        nc.vector.memset(zeros[:].bitcast(I32), 0)
+        nc.scalar.dma_start(out=rows[0:2, :], in_=d.rearrange("(g m) -> g m", g=2))
+        nc.scalar.dma_start(out=rows[2:4, :], in_=q.rearrange("(g m) -> g m", g=2))
+        nc.scalar.dma_start(out=rows[4:8, 0:PART], in_=k.rearrange("(j c) -> j c", j=4))
+        make_identity(nc, ident[:])
+        nc.sync.dma_start(out=a_raw[:], in_=a.rearrange("(p t) c -> p t c", t=SLOTS))
+        for g in (1, 0):
+            for pair in range(2):
+                load_z(g, pair)
+        u_rows = u.rearrange("(p t) n -> p t n", t=SLOTS)
+        for i in range(2):
+            nc.sync.dma_start(out=u_raw[0][:, :, cols(i, PIECE)], in_=u_rows[:, :, cols(i, PIECE)])
+        nc.sync.dma_start(out=u_raw[1][:], in_=u_rows[:, :, cols(1, PASS)])
 
-        def setup():
-            make_identity(nc, ident[:])
-            nc.scalar.activation(out=warm[:], in_=ident[:, 0:8], func=ACT.Relu)
+        for i, engine in enumerate(("scalar", "vector")):
+            interleave(engine, a_int[:, cols(i, SLOTS * PIECE)], a_raw[:, :, cols(i, PIECE)])
+        quantize(a_code[:], a_scale[:], a_int[:])
+        warm_up(5)
+        for g in (1, 0):
+            for pair in range(2):
+                turn_z(g, pair)
+        warm_up(2)
+        quantize_z(1)
+        turn_vectors()
+        interleave_u("vector", 0, PIECE)
+        quantize_z(0)
+        quantize_u(0, 1)
+        interleave_u("vector", PIECE, PIECE)
 
-        steps = {"load": load, "il_u": il_u, "q_u": q_u, "il_a": il_a, "q_a": q_a, "t_z": t_z, "e_z": e_z, "q_z": q_z, "m_s": m_s, "e_s": e_s, "q_s": q_s, "m_pay": m_pay, "e_pay": e_pay, "g_mean": g_mean, "t_d": t_d, "v_b": v_b, "t_b": t_b, "e_b": e_b, "q_b": q_b, "m_o0": m_o0, "m_o1": m_o1, "m_t0": m_t0, "m_t1": m_t1, "m_r": m_r, "e_r": e_r, "il_s": il_s, "g_q": g_q, "e_o": e_o, "e_t": e_t, "q_o": q_o, "st_o": st_o, "st_w": st_w, "st_s": st_s, "setup": setup}
-        for step in ORDER:
-            steps[step[0]](*step[1:])
+        for j in range(4):
+            multiply_pay(j, 1)
+        multiply_pay(0, 0)
+        multiply_s_chunk(0, 0)
+        multiply_pay(1, 0)
+        spread_d()
+        for j in range(3):
+            read_pay(j, 1)
+        read_s_chunk(0, 0)
+        quantize_u(1, 1)
+        for i in range(4):
+            interleave_u("gpsimd", PASS + i * PART, PART)
+        multiply_s_chunk(0, 1)
+        multiply_pay(2, 0)
+        multiply_s_slot(0, 0)
+        multiply_s_slot(0, 1)
+        read_pay(0, 0)
+        read_pay(1, 0)
+        read_s_chunk(0, 1)
+        multiply_s_slot(0, 2)
+        multiply_s_chunk(0, 2)
+        multiply_s_chunk(0, 3)
+        read_pay(2, 0)
+
+        mean_pay(0)
+        mean_pay(1)
+        make_b(0)
+        mean_pay(2)
+        make_b(1)
+        quantize_u(2, 2)
+        multiply_s_slot(0, 3)
+        read_s_slot(0, 0)
+        multiply_pay(3, 0)
+        read_s_slot(0, 1)
+        turn_b(0)
+        read_s_slot(0, 2)
+        turn_b(1)
+        read_s_slot(0, 3)
+        for i in range(2):
+            interleave_s("gpsimd", 0, i)
+
+        read_b(0)
+        multiply_s_chunk(1, 0)
+        read_s_chunk(0, 2)
+        multiply_s_slot(1, 0)
+        make_b(2)
+        read_pay(3, 1)
+        multiply_s_slot(1, 1)
+        read_pay(3, 0)
+        multiply_s_slot(1, 2)
+        read_s_chunk(0, 3)
+        turn_b(2)
+        read_s_slot(1, 0)
+        multiply_s_chunk(1, 1)
+        read_b(1)
+        multiply_s_chunk(1, 2)
+        read_s_slot(1, 1)
+        multiply_s_slot(1, 3)
+        read_s_slot(1, 2)
+        mean_pay(3)
+        make_b(3)
+        give("d")
+        turn_b(3)
+        read_b(2)
+        multiply_s_chunk(1, 3)
+        read_b(3)
+        read_s_slot(1, 3)
+        quantize_s(0, 0)
+        quantize_b(0)
+        quantize_s(1, 0)
+        for j in range(1, 4):
+            quantize_b(j)
+        interleave_s("vector", 1, 1)
+        interleave_s("gpsimd", 1, 0)
+
+        for g in range(2):
+            multiply_out(0, 0, g)
+            multiply_out_t(0, 0, g)
+        for j in range(3):
+            store_out("scalar", j, 0)
+            read_s_chunk(1, j)
+            for g in range(2):
+                multiply_out(j + 1, 0, g)
+            read_out_t("scalar", j, 0)
+            for g in range(2):
+                multiply_out_t(j + 1, 0, g)
+        quantize_s(0, 1)
+        read_s_chunk(1, 3)
+        read_out_t("scalar", 3, 0)
+
+        for j in range(3):
+            multiply_out_t(j, 1, 0)
+        for j in range(3):
+            multiply_out(j, 1, 0)
+        store_out("scalar", 3, 0)
+        quantize_s(1, 1)
+        store_codes(0, 0, 4)
+        for j in range(3):
+            multiply_out(j, 1, 1)
+        multiply_out(3, 1, 0)
+        multiply_out_t(0, 1, 1)
+        multiply_out_t(1, 1, 1)
+        multiply_out(3, 1, 1)
+        multiply_out_t(2, 1, 1)
+        for g in range(2):
+            multiply_out_t(3, 1, g)
+
+        store_out("scalar", 0, 1)
+        store_out("vector", 1, 1)
+        store_out("scalar", 2, 1)
+        read_out_t("scalar", 0, 1)
+        read_out_t("vector", 1, 1)
+        store_out("scalar", 3, 1)
+        read_out_t("vector", 2, 1)
+        store_codes(1, 0, 2)
+        read_out_t("scalar", 3, 1)
+        store_codes(1, 2, 2)
+        for quadrant in range(4):
+            store_scales(quadrant)

from contextlib import ExitStack

import concourse.mybir as mybir
from concourse.masks import make_identity

M, K, P, N = 1024, 512, 512, 1024
FLOPS = 2 * M * K * (P + N) + 2 * P * M * N
OUT_SCALE = 1.0 / 32

PART = 128
SLOTS = 4
PASS = PART * SLOTS
BANKS = 8
PIECE = 256

F32 = mybir.dt.float32
BF16 = mybir.dt.bfloat16
I32 = mybir.dt.int32
U32 = mybir.dt.uint32
U8 = mybir.dt.uint8
FP8X4 = mybir.dt.float8_e4m3fn_x4
ALU = mybir.AluOpType
ACT = mybir.ActivationFunctionType


def cols(i, width, count=1):
    return slice(width * i, width * (i + count))


def tile_likelihoodratiobachelierbasketdeltas_x1_kernel(tc, z, a, k, d, u, q, out_0, out_1, out_2):
    nc = tc.nc
    with ExitStack() as ctx:
        sb = ctx.enter_context(tc.tile_pool(name="sb", bufs=1))
        ps = ctx.enter_context(tc.psum_pool(name="ps", bufs=1))
        ctx.enter_context(tc.manual_schedule())

        def tile(name, shape, dtype):
            return sb.tile(shape, dtype, name=name, align_bytes=256)

        ident = tile("ident", [PART, PART], F32)
        zeros = tile("zeros", [PART, PASS], BF16)
        z_raw = tile("z_raw", [PART, 2, SLOTS, K], BF16)
        u_raw = [tile("u_raw%d" % h, [PART, SLOTS, PASS], BF16) for h in range(2)]
        a_raw = tile("a_raw", [PART, SLOTS, P], BF16)
        rows = tile("rows", [PART, PASS], BF16)
        rows_f32 = tile("rows_f32", [PART, PART], F32)
        vec = tile("vec", [PART, 8, 4], F32)
        q_f32 = tile("q_f32", [PART, 2, SLOTS], F32)
        z_int = tile("z_int", [PART, 2, SLOTS * PASS], BF16)
        u_int = tile("u_int", [PART, SLOTS * N], BF16)
        a_int = tile("a_int", [PART, SLOTS * P], BF16)
        z_code = tile("z_code", [PART, 2, PASS], U32)
        z_scale = tile("z_scale", [PART, 2, PASS], U8)
        u_code = tile("u_code", [PART, N], U32)
        u_scale = tile("u_scale", [PART, N], U8)
        a_code = tile("a_code", [PART, P], U32)
        a_scale = tile("a_scale", [PART, P], U8)
        pay = tile("pay", [PART, 4, M], F32)
        sums = tile("sums", [PART, 4, 2], F32)
        mean = [tile("mean%d" % j, [PART, 1], F32) for j in range(4)]
        b_rows = tile("b_rows", [PART, 4, M], BF16)
        b_int = tile("b_int", [PART, 4, 2 * SLOTS * PART], BF16)
        b_code = tile("b_code", [PART, 4, 2 * PART], U32)
        b_scale = tile("b_scale", [PART, 4, 2 * PART], U8)
        s_slots = tile("s_slots", [PART, 2, SLOTS, PASS], BF16)
        s_int = tile("s_int", [PART, 2, 2, SLOTS * PASS], BF16)
        s_code = tile("s_code", [PART, 2, 2, PASS], U32)
        s_scale = tile("s_scale", [PART, 2, 2, PASS], U8)
        o_f32 = tile("o_f32", [PART, 4, 2, PASS], F32)
        o_int = tile("o_int", [PART, 2, SLOTS * P], BF16)
        o_code = tile("o_code", [PART, 2, P], U32)
        o_scale = tile("o_scale", [PART, 2, P], U8)

        free = list(range(BANKS))
        held = {}

        def take(key):
            index = free.pop(0)
            held[key] = (index, ps.tile([PART, PASS], F32, name="bank", tag="bank%d" % index))
            return held[key][1]

        def give(key):
            index, bank = held[key]
            free.append(index)
            return bank

        def quantize(code, scale, interleaved):
            nc.vector.quantize_mx(out=code.bitcast(FP8X4), scales=scale, in_=interleaved)

        def mx(out, lhs_code, lhs_scale, rhs_code, rhs_scale, start, stop):
            nc.tensor.matmul_mx(out=out, lhsT=lhs_code.bitcast(FP8X4), lhsT_scale=lhs_scale,
                                rhs=rhs_code.bitcast(FP8X4), rhs_scale=rhs_scale, start=start, stop=stop)

        def interleave(engine, dst, src):
            if engine == "gpsimd":
                nc.gpsimd.tensor_scalar(out=dst.rearrange("p (c t) -> p c t", t=SLOTS), in0=src.rearrange("p t c -> p c t"),
                                        scalar1=1.0, scalar2=0.0, op0=ALU.mult, op1=ALU.add)
                return
            dst = dst.rearrange("p (c i t) -> p c t i", i=4, t=SLOTS)
            src = src.rearrange("p t (c i) -> p c t i", i=4)
            if engine == "vector":
                nc.vector.tensor_copy(out=dst, in_=src)
            else:
                nc.scalar.activation(out=dst, in_=src, func=ACT.Copy)

        def warm_up(count):
            bank = take("warm")
            for i in range(count):
                nc.tensor.matmul(out=bank[:], lhsT=zeros[:, 0:PART], rhs=zeros[:], start=True, stop=True)
            give("warm")

        def load_z(g, pair):
            src = z[cols(g, PASS), :].rearrange("(p t) k -> p t k", t=SLOTS)
            nc.sync.dma_start(out=z_raw[:, g, cols(pair, 2), :], in_=src[:, cols(pair, 2), :])

        def turn_z(g, pair):
            bank = take(("z", g, pair))
            for i in range(2):
                words = z_raw[:, g, 2 * pair + i, :].bitcast(F32)
                for w in range(2):
                    nc.tensor.transpose(bank[:, cols(2 * i + w, PART)], words[:, w : K // 2 : 2], ident[:])
            dst = z_int[:, g, cols(pair, 2 * PASS)].bitcast(F32).rearrange("p (i m w) -> p i m w", i=2, w=2)
            nc.scalar.copy(out=dst, in_=give(("z", g, pair))[:].rearrange("p (i w m) -> p i m w", i=2, w=2))

        def quantize_z(g):
            quantize(z_code[:, g, :], z_scale[:, g, :], z_int[:, g, :])

        def interleave_u(engine, first, width):
            h, start = divmod(first, PASS)
            interleave(engine, u_int[:, SLOTS * first : SLOTS * (first + width)], u_raw[h][:, :, start : start + width])

        def quantize_u(i, count):
            quantize(u_code[:, cols(i, PIECE, count)], u_scale[:, cols(i, PIECE, count)],
                     u_int[:, cols(i, SLOTS * PIECE, count)])

        def turn_vectors():
            nc.vector.tensor_copy(out=rows_f32[:], in_=rows[:, 0:PART])
            bank = take("vec")
            words = rows[:].bitcast(F32)
            for w in range(2):
                nc.tensor.transpose(bank[:, cols(w, PART)], words[:, w : PASS // 2 : 2], ident[:])
            nc.tensor.transpose(bank[:, cols(2, PART)], rows_f32[:], ident[:])
            src = give("vec")[:, 0 : 3 * PART].rearrange("p (s row) -> p row s", s=3)
            nc.scalar.copy(out=vec[:, :, 0:3], in_=src[:, 0:8, :])
            nc.gpsimd.tensor_copy(out=q_f32[:], in_=vec[:, 2:4, :].bitcast(BF16)[:, :, 0:SLOTS])

        def spread_d():
            bank = take("d")
            for g in range(2):
                for w in range(2):
                    nc.tensor.transpose(bank[:, cols(2 * g + w, PART)],
                                        vec[:, g, w : w + 1].to_broadcast([PART, PART]), ident[:])

        def multiply_pay(j, g):
            mx(take(("pay", j, g))[:], a_code[:, cols(j, PART)], a_scale[:, cols(j, PART)],
               z_code[:, g, :], z_scale[:, g, :], True, True)

        def read_pay(j, g):
            dst = pay[:, j, cols(g, PASS)].rearrange("p (w m e) -> p w m e", w=2, e=2)
            src = give(("pay", j, g))[:].rearrange("p (w e m) -> p w m e", w=2, e=2)
            nc.scalar.activation(out=dst, in_=src, func=ACT.Relu, bias=vec[:, 4 + j, 2:3],
                                 accum_out=sums[:, j, g : g + 1])

        def mean_pay(j):
            nc.vector.tensor_scalar(out=mean[j][:], in0=sums[:, j, 0:1], scalar1=sums[:, j, 1:2], scalar2=1.0 / M,
                                    op0=ALU.add, op1=ALU.mult)

        def make_b(j):
            nc.vector.scalar_tensor_tensor(out=b_rows[:, j, :], in0=pay[:, j, :], scalar=mean[j][:],
                                           in1=held["d"][1][:].bitcast(BF16), op0=ALU.subtract, op1=ALU.mult)

        def turn_b(j):
            bank = take(("b", j))
            words = b_rows[:, j, :].bitcast(F32)
            for i in range(4):
                nc.tensor.transpose(bank[:, cols(i, PART)], words[:, cols(i, PART)], ident[:])

        def read_b(j):
            dst = b_int[:, j, :].bitcast(F32).rearrange("p (g c w) -> p g c w", g=2, w=2)
            nc.scalar.copy(out=dst, in_=give(("b", j))[:].rearrange("p (g w c) -> p g c w", g=2, w=2))

        def quantize_b(j):
            quantize(b_code[:, j, :], b_scale[:, j, :], b_int[:, j, :])

        def multiply_s_chunk(h, c):
            bank = take(("s", h, c))
            n = cols(4 * h + c, PART)
            for t in range(SLOTS):
                m = cols(t, PART)
                mx(bank[:, m], z_code[:, h, m], z_scale[:, h, m], u_code[:, n], u_scale[:, n], True, True)

        def read_s_chunk(h, c):
            dst = s_int[:, h, h, :].rearrange("p (r n t) -> p r n t", r=SLOTS, t=SLOTS)[:, :, cols(c, PART // SLOTS), :]
            src = give(("s", h, c))[:].rearrange("p (t n r) -> p r n t", t=SLOTS, r=SLOTS)
            factor = vec[:, 2 + h, 0:2].bitcast(BF16).unsqueeze(1).unsqueeze(1)
            nc.vector.tensor_tensor(out=dst, in0=src, in1=factor.to_broadcast([PART, SLOTS, PART // SLOTS, SLOTS]),
                                    op=ALU.mult)

        def multiply_s_slot(h, t):
            m, n = cols(t, PART), cols(h, PASS)
            mx(take(("slot", h, t))[:], z_code[:, 1 - h, m], z_scale[:, 1 - h, m], u_code[:, n], u_scale[:, n], True, True)

        def read_s_slot(h, t):
            nc.scalar.activation(out=s_slots[:, h, t, :].rearrange("p (r n) -> p r n", r=SLOTS),
                                 in_=give(("slot", h, t))[:].rearrange("p (n r) -> p r n", r=SLOTS),
                                 func=ACT.Copy, scale=q_f32[:, 1 - h, t : t + 1])

        def interleave_s(engine, h, i):
            interleave(engine, s_int[:, h, 1 - h, cols(i, SLOTS * PIECE)], s_slots[:, h, :, cols(i, PIECE)])

        def quantize_s(g, h):
            quantize(s_code[:, h, g, :], s_scale[:, h, g, :], s_int[:, h, g, :])

        def multiply_out(j, h, g):
            bank = take(("out", j, h)) if g == 0 else held[("out", j, h)][1]
            c = cols(g, PART)
            mx(bank[:], b_code[:, j, c], b_scale[:, j, c], s_code[:, h, g, :], s_scale[:, h, g, :], g == 0, g == 1)

        def multiply_out_t(j, h, g):
            bank = take(("out_t", j, h)) if g == 0 else held[("out_t", j, h)][1]
            c = cols(g, PART)
            for r in range(SLOTS):
                n = cols(r, PART)
                mx(bank[:, n], s_code[:, h, g, n], s_scale[:, h, g, n], b_code[:, j, c], b_scale[:, j, c],
                   g == 0 and r == 0, g == 1 and r == SLOTS - 1)

        def scaled_copy(engine, dst, src):
            if engine == "vector":
                nc.vector.tensor_scalar(out=dst, in0=src, scalar1=OUT_SCALE, scalar2=None, op0=ALU.mult)
            else:
                nc.scalar.activation(out=dst, in_=src, func=ACT.Copy, scale=OUT_SCALE)

        def store_out(engine, j, h):
            scaled_copy(engine, o_f32[:, j, h, :].rearrange("p (n r) -> p n r", r=SLOTS),
                        give(("out", j, h))[:].rearrange("p (r n) -> p n r", r=SLOTS))
            nc.sync.dma_start(out=out_0[cols(j, PART), cols(h, PASS)], in_=o_f32[:, j, h, :])

        def read_out_t(engine, j, h):
            scaled_copy(engine, o_int[:, h, cols(j, PASS)].rearrange("p (c r) -> p c r", r=SLOTS),
                        give(("out_t", j, h))[:].rearrange("p (r c) -> p c r", r=SLOTS))

        def store_codes(h, j, count):
            c = cols(j, PART, count)
            quantize(o_code[:, h, c], o_scale[:, h, c], o_int[:, h, cols(j, PASS, count)])
            dst = out_1[h].rearrange("p m r -> p (m r)").bitcast(I32)
            nc.sync.dma_start(out=dst[:, c], in_=o_code[:, h, c].bitcast(I32))

        def store_scales(quadrant):
            dst = out_2[:, cols(quadrant, 4), :].rearrange("h row m -> row h m").bitcast(I32)
            queue = nc.sync if quadrant % 2 == 0 else nc.scalar
            queue.dma_start(out=dst, in_=o_scale[32 * quadrant : 32 * quadrant + 4, :, :].bitcast(I32))


        nc.gpsimd.memset(rows[:].bitcast(I32), 0)
        nc.vector.memset(zeros[:].bitcast(I32), 0)
        nc.scalar.dma_start(out=rows[0:2, :], in_=d.rearrange("(g m) -> g m", g=2))
        nc.scalar.dma_start(out=rows[2:4, :], in_=q.rearrange("(g m) -> g m", g=2))
        nc.scalar.dma_start(out=rows[4:8, 0:PART], in_=k.rearrange("(j c) -> j c", j=4))
        make_identity(nc, ident[:])
        nc.sync.dma_start(out=a_raw[:], in_=a.rearrange("(p t) c -> p t c", t=SLOTS))
        for g in (1, 0):
            for pair in range(2):
                load_z(g, pair)
        u_rows = u.rearrange("(p t) n -> p t n", t=SLOTS)
        for i in range(2):
            nc.sync.dma_start(out=u_raw[0][:, :, cols(i, PIECE)], in_=u_rows[:, :, cols(i, PIECE)])
        nc.sync.dma_start(out=u_raw[1][:], in_=u_rows[:, :, cols(1, PASS)])

        for i, engine in enumerate(("scalar", "vector")):
            interleave(engine, a_int[:, cols(i, SLOTS * PIECE)], a_raw[:, :, cols(i, PIECE)])
        quantize(a_code[:], a_scale[:], a_int[:])
        warm_up(5)
        for g in (1, 0):
            for pair in range(2):
                turn_z(g, pair)
        warm_up(2)
        quantize_z(1)
        turn_vectors()
        interleave_u("vector", 0, PIECE)
        quantize_z(0)
        quantize_u(0, 1)
        interleave_u("vector", PIECE, PIECE)

        for j in range(4):
            multiply_pay(j, 1)
        multiply_pay(0, 0)
        multiply_s_chunk(0, 0)
        multiply_pay(1, 0)
        spread_d()
        for j in range(3):
            read_pay(j, 1)
        read_s_chunk(0, 0)
        quantize_u(1, 1)
        for i in range(4):
            interleave_u("gpsimd", PASS + i * PART, PART)
        multiply_s_chunk(0, 1)
        multiply_pay(2, 0)
        multiply_s_slot(0, 0)
        multiply_s_slot(0, 1)
        read_pay(0, 0)
        read_pay(1, 0)
        read_s_chunk(0, 1)
        multiply_s_slot(0, 2)
        multiply_s_chunk(0, 2)
        multiply_s_chunk(0, 3)
        read_pay(2, 0)

        mean_pay(0)
        mean_pay(1)
        make_b(0)
        mean_pay(2)
        make_b(1)
        quantize_u(2, 2)
        multiply_s_slot(0, 3)
        read_s_slot(0, 0)
        multiply_pay(3, 0)
        read_s_slot(0, 1)
        turn_b(0)
        read_s_slot(0, 2)
        turn_b(1)
        read_s_slot(0, 3)
        for i in range(2):
            interleave_s("gpsimd", 0, i)

        read_b(0)
        multiply_s_chunk(1, 0)
        read_s_chunk(0, 2)
        multiply_s_slot(1, 0)
        make_b(2)
        read_pay(3, 1)
        multiply_s_slot(1, 1)
        read_pay(3, 0)
        multiply_s_slot(1, 2)
        read_s_chunk(0, 3)
        turn_b(2)
        read_s_slot(1, 0)
        multiply_s_chunk(1, 1)
        read_b(1)
        multiply_s_chunk(1, 2)
        read_s_slot(1, 1)
        multiply_s_slot(1, 3)
        read_s_slot(1, 2)
        mean_pay(3)
        make_b(3)
        give("d")
        turn_b(3)
        read_b(2)
        multiply_s_chunk(1, 3)
        read_b(3)
        read_s_slot(1, 3)
        quantize_s(0, 0)
        quantize_b(0)
        quantize_s(1, 0)
        for j in range(1, 4):
            quantize_b(j)
        interleave_s("vector", 1, 1)
        interleave_s("gpsimd", 1, 0)

        for g in range(2):
            multiply_out(0, 0, g)
            multiply_out_t(0, 0, g)
        for j in range(3):
            store_out("scalar", j, 0)
            read_s_chunk(1, j)
            for g in range(2):
                multiply_out(j + 1, 0, g)
            read_out_t("scalar", j, 0)
            for g in range(2):
                multiply_out_t(j + 1, 0, g)
        quantize_s(0, 1)
        read_s_chunk(1, 3)
        read_out_t("scalar", 3, 0)

        for j in range(3):
            multiply_out_t(j, 1, 0)
        for j in range(3):
            multiply_out(j, 1, 0)
        store_out("scalar", 3, 0)
        quantize_s(1, 1)
        store_codes(0, 0, 4)
        for j in range(3):
            multiply_out(j, 1, 1)
        multiply_out(3, 1, 0)
        multiply_out_t(0, 1, 1)
        multiply_out_t(1, 1, 1)
        multiply_out(3, 1, 1)
        multiply_out_t(2, 1, 1)
        for g in range(2):
            multiply_out_t(3, 1, g)

        store_out("scalar", 0, 1)
        store_out("vector", 1, 1)
        store_out("scalar", 2, 1)
        read_out_t("scalar", 0, 1)
        read_out_t("vector", 1, 1)
        store_out("scalar", 3, 1)
        read_out_t("vector", 2, 1)
        store_codes(1, 0, 2)
        read_out_t("scalar", 3, 1)
        store_codes(1, 2, 2)
        for quadrant in range(4):
            store_scales(quadrant)
